import numpy as np
import ml_dtypes

BF16 = ml_dtypes.bfloat16


def bf(x):
    return np.asarray(x, np.float32).astype(BF16)


def f32(x):
    return np.asarray(x, np.float32)


def f64(x):
    return np.asarray(x).astype(np.float64)


def striped(idx):
    return np.concatenate([l.reshape(-1, 16).T for l in idx])


def rows(idx, k):
    return np.tile(np.repeat(idx, 16, axis=0), (k // (16 * 8), 1))


def look(tab, idx):
    return np.take_along_axis(f64(tab), rows(idx, len(tab)), axis=1)


K, S, V, N = 128, 2048, 1024, 1024


def setup_inputs():
    return {"tab": f32(np.random.standard_normal((2, K, S))), "y": f32(np.random.standard_normal((K, V))), "offs": striped(np.stack([np.random.permutation(S)[:N] for _ in range(8)]))}


def reference(tab, y, offs):
    idx = np.stack([g.T.reshape(-1) for g in np.split(offs, 8)])
    x = (look(tab[0], idx) * f64(y)) * (1.0 / (1.0 + np.exp(-look(tab[1], idx))))
    return x

@@ -1,0 +1,38 @@
+import concourse.mybir as mybir
+
+F32, U16 = mybir.dt.float32, mybir.dt.uint16
+SIGMOID = mybir.ActivationFunctionType.Sigmoid
+MULT = mybir.AluOpType.mult
+
+P = 128
+ENTRIES_A_COLUMN = 16
+PIECE = 512
+
+
+def tile_lookup_vg_mulsig_out_kernel(tc, tab, y, offs, out):
+    nc = tc.nc
+    places = tab.shape[2]
+    n = y.shape[1]
+    with (
+        tc.tile_pool(name="held", bufs=1) as held,
+        tc.tile_pool(name="work", bufs=2) as work,
+    ):
+        offsets = held.tile([P, n // ENTRIES_A_COLUMN], U16)
+        gates = held.tile([P, places], F32)
+        stream = held.tile([P, n], F32)
+        values = held.tile([P, places], F32)
+        nc.sync.dma_start(offsets[:], offs)
+        nc.sync.dma_start(gates[:], tab[1])
+        nc.sync.dma_start(stream[:], y)
+        nc.sync.dma_start(values[:], tab[0])
+
+        for start in range(0, n, PIECE):
+            columns = slice(start, start + PIECE)
+            piece = offsets[:, start // ENTRIES_A_COLUMN : (start + PIECE) // ENTRIES_A_COLUMN]
+            opened = work.tile([P, PIECE], F32)
+            product = work.tile([P, PIECE], F32)
+            result = work.tile([P, PIECE], F32)
+            nc.scalar.activation(opened[:], gates[:].indirect(piece), SIGMOID)
+            nc.vector.tensor_tensor(product[:], values[:].indirect(piece), stream[:, columns], MULT)
+            nc.vector.tensor_tensor(result[:], product[:], opened[:], MULT)
+            nc.sync.dma_start(out[:, columns], result[:])

@@ -8,6 +8,9 @@ P = 128
 ENTRIES_A_COLUMN = 16
 PIECE = 512
 
+def entries(offsets, start):
+    return offsets[:, start // ENTRIES_A_COLUMN : (start + PIECE) // ENTRIES_A_COLUMN]
+
 
 def tile_lookup_vg_mulsig_out_kernel(tc, tab, y, offs, out):
     nc = tc.nc
@@ -21,18 +24,25 @@ def tile_lookup_vg_mulsig_out_kernel(tc, tab, y, offs, out):
         gates = held.tile([P, places], F32)
         stream = held.tile([P, n], F32)
         values = held.tile([P, places], F32)
+
+        warm_up = held.tile([P, 1], F32)
+        nc.vector.memset(warm_up[:], 0.0)
+        warmed = held.tile([P, 1], F32)
+        nc.scalar.activation(warmed[:], warm_up[:], SIGMOID)
+
         nc.sync.dma_start(offsets[:], offs)
         nc.sync.dma_start(gates[:], tab[1])
         nc.sync.dma_start(stream[:], y)
         nc.sync.dma_start(values[:], tab[0])
 
+        gated_streams = []
         for start in range(0, n, PIECE):
-            columns = slice(start, start + PIECE)
-            piece = offsets[:, start // ENTRIES_A_COLUMN : (start + PIECE) // ENTRIES_A_COLUMN]
             opened = work.tile([P, PIECE], F32)
-            product = work.tile([P, PIECE], F32)
+            gated_stream = work.tile([P, PIECE], F32)
+            nc.scalar.activation(opened[:], gates[:].indirect(entries(offsets, start)), SIGMOID)
+            nc.vector.tensor_tensor(gated_stream[:], opened[:], stream[:, start : start + PIECE], MULT)
+            gated_streams.append(gated_stream)
+        for start, gated_stream in zip(range(0, n, PIECE), gated_streams):
             result = work.tile([P, PIECE], F32)
-            nc.scalar.activation(opened[:], gates[:].indirect(piece), SIGMOID)
-            nc.vector.tensor_tensor(product[:], values[:].indirect(piece), stream[:, columns], MULT)
-            nc.vector.tensor_tensor(result[:], product[:], opened[:], MULT)
-            nc.sync.dma_start(out[:, columns], result[:])
+            nc.vector.tensor_tensor(result[:], values[:].indirect(entries(offsets, start)), gated_stream[:], MULT)
+            nc.sync.dma_start(out[:, start : start + PIECE], result[:])

@@ -6,10 +6,12 @@ MULT = mybir.AluOpType.mult
 
 P = 128
 ENTRIES_A_COLUMN = 16
-PIECE = 512
+GATE_PIECE = 512
+VALUE_PIECE = 256
 
-def entries(offsets, start):
-    return offsets[:, start // ENTRIES_A_COLUMN : (start + PIECE) // ENTRIES_A_COLUMN]
+
+def entries(offsets, start, count):
+    return offsets[:, start // ENTRIES_A_COLUMN : (start + count) // ENTRIES_A_COLUMN]
 
 
 def tile_lookup_vg_mulsig_out_kernel(tc, tab, y, offs, out):
@@ -19,6 +21,7 @@ def tile_lookup_vg_mulsig_out_kernel(tc, tab, y, offs, out):
     with (
         tc.tile_pool(name="held", bufs=1) as held,
         tc.tile_pool(name="work", bufs=2) as work,
+        tc.tile_pool(name="results", bufs=4) as results,
     ):
         offsets = held.tile([P, n // ENTRIES_A_COLUMN], U16)
         gates = held.tile([P, places], F32)
@@ -35,14 +38,15 @@ def tile_lookup_vg_mulsig_out_kernel(tc, tab, y, offs, out):
         nc.sync.dma_start(stream[:], y)
         nc.sync.dma_start(values[:], tab[0])
 
-        gated_streams = []
-        for start in range(0, n, PIECE):
-            opened = work.tile([P, PIECE], F32)
-            gated_stream = work.tile([P, PIECE], F32)
-            nc.scalar.activation(opened[:], gates[:].indirect(entries(offsets, start)), SIGMOID)
-            nc.vector.tensor_tensor(gated_stream[:], opened[:], stream[:, start : start + PIECE], MULT)
-            gated_streams.append(gated_stream)
-        for start, gated_stream in zip(range(0, n, PIECE), gated_streams):
-            result = work.tile([P, PIECE], F32)
-            nc.vector.tensor_tensor(result[:], values[:].indirect(entries(offsets, start)), gated_stream[:], MULT)
-            nc.sync.dma_start(out[:, start : start + PIECE], result[:])
+        gated_stream = held.tile([P, n], F32)
+        for start in range(0, n, GATE_PIECE):
+            columns = slice(start, start + GATE_PIECE)
+            opened = work.tile([P, GATE_PIECE], F32)
+            nc.scalar.activation(opened[:], gates[:].indirect(entries(offsets, start, GATE_PIECE)), SIGMOID)
+            nc.vector.tensor_tensor(gated_stream[:, columns], opened[:], stream[:, columns], MULT)
+        for start in range(0, n, VALUE_PIECE):
+            columns = slice(start, start + VALUE_PIECE)
+            result = results.tile([P, VALUE_PIECE], F32)
+            piece = entries(offsets, start, VALUE_PIECE)
+            nc.vector.tensor_tensor(result[:], values[:].indirect(piece), gated_stream[:, columns], MULT)
+            nc.sync.dma_start(out[:, columns], result[:])

import concourse.mybir as mybir

F32, U16 = mybir.dt.float32, mybir.dt.uint16
SIGMOID = mybir.ActivationFunctionType.Sigmoid
MULT = mybir.AluOpType.mult

P = 128
ENTRIES_A_COLUMN = 16
GATE_PIECE = 512
VALUE_PIECE = 256


def entries(offsets, start, count):
    return offsets[:, start // ENTRIES_A_COLUMN : (start + count) // ENTRIES_A_COLUMN]


def tile_lookup_vg_mulsig_out_kernel(tc, tab, y, offs, out):
    nc = tc.nc
    places = tab.shape[2]
    n = y.shape[1]
    with (
        tc.tile_pool(name="held", bufs=1) as held,
        tc.tile_pool(name="work", bufs=2) as work,
        tc.tile_pool(name="results", bufs=4) as results,
    ):
        offsets = held.tile([P, n // ENTRIES_A_COLUMN], U16)
        gates = held.tile([P, places], F32)
        stream = held.tile([P, n], F32)
        values = held.tile([P, places], F32)

        warm_up = held.tile([P, 1], F32)
        nc.vector.memset(warm_up[:], 0.0)
        warmed = held.tile([P, 1], F32)
        nc.scalar.activation(warmed[:], warm_up[:], SIGMOID)

        nc.sync.dma_start(offsets[:], offs)
        nc.sync.dma_start(gates[:], tab[1])
        nc.sync.dma_start(stream[:], y)
        nc.sync.dma_start(values[:], tab[0])

        gated_stream = held.tile([P, n], F32)
        for start in range(0, n, GATE_PIECE):
            columns = slice(start, start + GATE_PIECE)
            opened = work.tile([P, GATE_PIECE], F32)
            nc.scalar.activation(opened[:], gates[:].indirect(entries(offsets, start, GATE_PIECE)), SIGMOID)
            nc.vector.tensor_tensor(gated_stream[:, columns], opened[:], stream[:, columns], MULT)
        for start in range(0, n, VALUE_PIECE):
            columns = slice(start, start + VALUE_PIECE)
            result = results.tile([P, VALUE_PIECE], F32)
            piece = entries(offsets, start, VALUE_PIECE)
            nc.vector.tensor_tensor(result[:], values[:].indirect(piece), gated_stream[:, columns], MULT)
            nc.sync.dma_start(out[:, columns], result[:])
